import numpy as np
import ml_dtypes


def mxq(x, axis, fmt="e4m3"):
    dtype, down = {"e4m3": (ml_dtypes.float8_e4m3fn, 7), "e5m2": (ml_dtypes.float8_e5m2, 14)}[fmt]
    v = np.moveaxis(np.asarray(x, np.float32).astype(ml_dtypes.bfloat16).astype(np.float64), axis, -1)
    blocks = v.reshape(v.shape[:-1] + (-1, 32))
    amax = np.abs(blocks).max(-1, keepdims=True)
    byte = np.maximum(np.where(amax > 0, np.frexp(amax)[1] - 1 + 127, 0) - down, 1)
    scale = np.exp2(byte - 127.0)
    codes = (blocks / scale).astype(np.float32).astype(dtype).astype(np.float64)
    return np.moveaxis((codes * scale).reshape(v.shape), -1, axis)


WIDE = False


def mx_kscale(k):
    if not WIDE:
        return np.ones(k)
    levels = np.array([10, -10, 5, -5, 0])
    if k % 512:
        return np.exp2(np.random.permutation(np.resize(levels, k // 32))).repeat(32)
    a = np.empty((k // 512, 16))
    for p in range(k // 512):
        a[p, :8] = np.random.permutation(np.resize(levels, 8))
        for g in range(8):
            far = levels[np.abs(levels - a[p, g]) >= 10]
            a[p, g + 8] = far[np.random.randint(len(far))]
    return np.exp2(a.ravel()).repeat(32)


def f64(x):
    return np.asarray(x).astype(np.float64)


def striped(idx):
    return np.tile(idx.reshape(-1, 16).T, (8, 1)).astype(np.uint16)


def unstriped(offs):
    return offs[:16].T.reshape(-1).astype(np.int64)


def striped8(idx):
    return np.concatenate([x.reshape(-1, 16).T for x in idx]).astype(np.uint16)


def runs(offs, k):
    lists = np.stack([offs[16 * r : 16 * r + 16].T.reshape(-1) for r in range(8)]).astype(np.int64)
    return lists[np.arange(k) % 512 // 64]


def pack_weight(w):
    k, n = w.shape
    w = f64(np.asarray(w, np.float32).astype(ml_dtypes.bfloat16)).reshape(k // 32, 32, n)
    amax = np.abs(w).max(1)
    byte = np.clip(np.where(amax > 0, np.frexp(amax)[1] - 1 + 127 - 7, 1), 1, 254)
    scaled = (w * np.exp2(127.0 - byte)[:, None, :]).reshape(k, n).astype(np.float32)
    words = np.ascontiguousarray(scaled.reshape(k // 512, 128, 4, n).transpose(0, 1, 3, 2)).astype(ml_dtypes.float8_e4m3fn).view(np.uint8)
    return words, np.ascontiguousarray(byte.astype(np.uint8).reshape(k // 512, 16, n))


def unpack_weight(words, scales):
    g, p, n, _ = words.shape
    vals = np.ascontiguousarray(words).view(ml_dtypes.float8_e4m3fn).astype(np.float64) * np.repeat(np.exp2(scales.astype(np.float64) - 127.0), 8, axis=1)[..., None]
    return vals.transpose(0, 1, 3, 2).reshape(g * 512, n)


def sigmoid(v):
    return 1.0 / (1.0 + np.exp(-np.maximum(v, -700.0)))

def planes(y):
    n, m = y.shape
    v = y.astype(np.float32).astype(ml_dtypes.bfloat16).astype(np.float64).reshape(n // 32, 32, m)
    top = np.abs(v).max(1)
    byte = np.clip(np.where(top > 0, np.frexp(top)[1] - 1 + 127 - 7, 1), 1, 254)
    codes = (v * np.exp2(127.0 - byte)[:, None, :]).reshape(n, m).astype(np.float32).astype(ml_dtypes.float8_e4m3fn).view(np.uint8)
    words = codes.reshape(n // 512, 128, 4, m).transpose(0, 1, 3, 2)
    return np.ascontiguousarray(words), np.ascontiguousarray(byte.astype(np.uint8).reshape(n // 512, 16, m))


K, T, S, N, H = 512, 2048, 512, 512, 512


def setup_inputs():
    n = np.random.standard_normal
    s = mx_kscale(K)[:, None]
    u = mx_kscale(S)
    packed_xT = pack_weight(n((K, T)) * s)
    packed_w1 = pack_weight(n((S, N)) / np.sqrt(S) / u[:, None])
    return {
        "x_words": packed_xT[0],
        "x_scales": packed_xT[1],
        "wa": (n((K, H)) / np.sqrt(K) / s).astype(np.float32),
        "gt": (np.random.uniform(0.5, 1.5, (S, 1)) * u[:, None]).astype(np.float32),
        "w1_words": packed_w1[0],
        "w1_scales": packed_w1[1],
        "offs": striped(np.random.permutation(T)[:S]),
        "n1": striped8(np.stack([np.random.permutation(H) for _ in range(8)])),
        "n2": striped8(np.stack([np.random.permutation(H) for _ in range(8)])),
        "n3": striped8(np.stack([np.random.permutation(H) for _ in range(8)])),
        "n4": striped8(np.stack([np.random.permutation(H) for _ in range(8)])),
    }


def reference(x_words, x_scales, wa, gt, w1_words, w1_scales, offs, n1, n2, n3, n4):
    xq = unpack_weight(x_words, x_scales)[:, unstriped(offs)]
    y = xq.T @ mxq(f64(wa), 0, "e4m3")
    z = f64(gt) * (np.minimum(np.maximum(y, y[np.arange(S)[:, None], runs(n1, S)]), y[np.arange(S)[:, None], runs(n2, S)]))
    h = unpack_weight(w1_words, w1_scales).T @ mxq(z, 0, "e4m3")
    out_0 = h + (sigmoid(h[np.arange(N)[:, None], runs(n3, N)])) * (h[np.arange(N)[:, None], runs(n4, N)] - h)
    return (out_0,) + planes(out_0)

@@ -1,0 +1,202 @@
+from contextlib import ExitStack
+
+import concourse.mybir as mybir
+
+K, T, S, N, H = 512, 2048, 512, 512, 512
+FLOPS = 2 * K * S * H + 2 * S * N * H
+
+F32 = mybir.dt.float32
+BF16 = mybir.dt.bfloat16
+I32 = mybir.dt.int32
+U32 = mybir.dt.uint32
+U16 = mybir.dt.uint16
+U8 = mybir.dt.uint8
+FP8X4 = mybir.dt.float8_e4m3fn_x4
+ALU = mybir.AluOpType
+ACT = mybir.ActivationFunctionType
+
+P = 128
+PACK = 4
+WA_CHUNKS = ((0, 256), (256, 256))
+Z_CHUNKS = ((0, 256), (256, 128), (384, 128))
+OUT_CHUNKS = ((0, 256), (256, 128), (384, 128))
+
+
+def tile_picked_tokminmxtrack_none_po_kernel(
+    tc, x_words, x_scales, wa, gt, w1_words, w1_scales, offs, n1, n2, n3, n4, out_0, out_1, out_2
+):
+    nc = tc.nc
+    with ExitStack() as ctx:
+        keep = ctx.enter_context(tc.tile_pool(name="keep", bufs=1))
+        psum = ctx.enter_context(tc.psum_pool(name="psum", bufs=1))
+
+        def sb(name, shape, dtype, tag=None):
+            return keep.tile(shape, dtype, name=name, tag=tag or name, align_bytes=64)
+
+        def load_list(name, src):
+            tile = keep.tile([P, S // 16], U16, name=name)
+            nc.sync.dma_start(tile[:], src)
+            return tile
+
+        def part(lists, c0, width):
+            return lists[:, c0 // 16 : (c0 + width) // 16]
+
+        def load_scale_rows(queue, tile, rows):
+            by_row = rows.rearrange("(q r) c -> r q c", r=PACK)
+            for r in range(PACK):
+                queue.dma_start(tile[r:P:32, :].bitcast(I32), by_row[r].bitcast(I32))
+
+        def interleave(copy, dst, src):
+            copy(dst.rearrange("p (c i) t -> p c t i", i=4), src.rearrange("p t (c i) -> p c t i", i=4))
+
+        def quantize(codes, scales, woven):
+            nc.vector.quantize_mx(out=codes.bitcast(FP8X4), scales=scales, in_=woven.rearrange("p c t -> p (c t)"))
+
+        x_bytes = sb("x_bytes", [P, T], U8)
+        nc.vector.memset(x_bytes[:].bitcast(I32), 0)
+        offs_sb = load_list("offs_sb", offs)
+        x_codes = sb("x_codes", [P, T], U32)
+        nc.sync.dma_start(x_codes[:].bitcast(I32), x_words[0].rearrange("p c r -> p (c r)").bitcast(I32))
+        load_scale_rows(nc.sync, x_bytes, x_scales[0])
+        wa_rows = wa.rearrange("(p t) c -> p t c", t=PACK)
+        wa_raw = []
+        for i, (c0, width) in enumerate(WA_CHUNKS):
+            raw = sb("wa_raw%d" % i, [P, PACK, width], F32)
+            nc.sync.dma_start(raw[:], wa_rows[:, :, c0 : c0 + width])
+            wa_raw.append(raw)
+
+        warm = sb("warm", [P, 2], F32)
+        nc.vector.memset(warm[:, 0:1], 0.0)
+        nc.scalar.activation(warm[:, 1:2], warm[:, 0:1], ACT.Sigmoid)
+
+        w1_bytes = sb("w1_bytes", [P, N], U8)
+        nc.vector.memset(w1_bytes[:].bitcast(I32), 0)
+        gate = sb("gate", [P, PACK], F32)
+        nc.sync.dma_start(gate[:], gt.rearrange("(p t) o -> p (t o)", t=PACK))
+        n1_sb = load_list("n1_sb", n1)
+        n2_sb = load_list("n2_sb", n2)
+        w1_codes = sb("w1_codes", [P, N], U32)
+        nc.sync.dma_start(w1_codes[:].bitcast(I32), w1_words[0].rearrange("p c r -> p (c r)").bitcast(I32))
+        load_scale_rows(nc.sync, w1_bytes, w1_scales[0])
+        n3_sb = load_list("n3_sb", n3)
+        n4_sb = load_list("n4_sb", n4)
+
+        gate_abs = sb("gate_abs", [P, PACK], F32)
+        gate_sign = sb("gate_sign", [P, PACK], F32)
+        nc.scalar.activation(gate_abs[:], gate[:], ACT.Abs)
+        nc.scalar.activation(gate_sign[:], gate[:], ACT.Sign)
+
+        tok_bytes = sb("tok_bytes", [P, S], U8)
+        nc.vector.tensor_copy(tok_bytes[:], x_bytes[:].indirect(offs_sb[:]))
+        tok_codes = sb("tok_codes", [P, S], U32)
+        nc.vector.tensor_copy(tok_codes[:].rearrange("p (t m) -> p m t", t=PACK), x_codes[:].indirect(offs_sb[:]))
+        tok_scales = sb("tok_scales", [P, S], U8)
+        nc.vector.tensor_copy(
+            tok_scales[:].rearrange("p (t m) -> p t m", t=PACK), tok_bytes[:].rearrange("p (m t) -> p t m", t=PACK)
+        )
+
+        y_win = [sb("y_win%d" % t, [P, H], F32) for t in range(PACK)]
+        y_own = [sb("y_own%d" % i, [P, PACK, w], BF16) for i, (c0, w) in enumerate(WA_CHUNKS)]
+        y_ps = {}
+        for i, (c0, width) in enumerate(WA_CHUNKS):
+            woven = sb("wa_woven%d" % i, [P, width, PACK], BF16)
+            copy = nc.vector.tensor_copy if i == len(WA_CHUNKS) - 1 else nc.scalar.copy
+            interleave(copy, woven[:], wa_raw[i][:])
+            codes = sb("wa_codes%d" % i, [P, width], U32)
+            scales = sb("wa_scales%d" % i, [P, width], U8)
+            quantize(codes[:], scales[:], woven[:])
+            for t in range(PACK):
+                cols = slice(t * P, (t + 1) * P)
+                acc = psum.tile([P, width], F32, name="y_ps", tag="bank%d" % (2 * t + i))
+                nc.tensor.matmul_mx(
+                    out=acc[:], lhsT=tok_codes[:, cols].bitcast(FP8X4), lhsT_scale=tok_scales[:, cols],
+                    rhs=codes[:].bitcast(FP8X4), rhs_scale=scales[:], start=True, stop=True,
+                )
+                y_ps[t, i] = acc
+            for t in range(PACK):
+                nc.scalar.activation(
+                    y_win[t][:, c0 : c0 + width], y_ps[t, i][:], ACT.Copy, scale=gate_abs[:, t : t + 1]
+                )
+        for i in range(len(WA_CHUNKS)):
+            for t in range(PACK):
+                nc.scalar.activation(y_own[i][:, t, :], y_ps[t, i][:], ACT.Copy, scale=gate_abs[:, t : t + 1])
+
+        w1_dealt = sb("w1_dealt", [P, N], U32)
+        nc.vector.tensor_copy(
+            w1_dealt[:].bitcast(I32).rearrange("p (t m) -> p m t", t=PACK),
+            w1_codes[:].bitcast(I32).rearrange("p (m t) -> p m t", t=PACK),
+        )
+        w1_sc = sb("w1_sc", [P, N], U8)
+        nc.vector.tensor_copy(
+            w1_sc[:].rearrange("p (t m) -> p t m", t=PACK), w1_bytes[:].rearrange("p (m t) -> p t m", t=PACK)
+        )
+
+        h_win = [sb("h_win%d" % t, [P, H], F32) for t in range(PACK)]
+        h_ps = [psum.tile([P, H], F32, name="h_ps", tag="bank%d" % (2 * t)) for t in range(PACK)]
+        for i, (c0, width) in enumerate(Z_CHUNKS):
+            last = i == len(Z_CHUNKS) - 1
+            first = sb("first%d" % i, [P, PACK, width], BF16, tag="first")
+            second = sb("second%d" % i, [P, PACK, width], BF16, tag="z_woven0" if last else "second")
+            for t in range(PACK):
+                nc.vector.tensor_copy(first[:, t, :], y_win[t][:].indirect(part(n1_sb, c0, width)))
+                if not last:
+                    nc.vector.tensor_copy(second[:, t, :], y_win[t][:].indirect(part(n2_sb, c0, width)))
+            own = y_own[c0 // 256][:, :, c0 % 256 : c0 % 256 + width]
+            larger = sb("larger%d" % i, [P, PACK, width], BF16)
+            nc.vector.tensor_tensor(larger[:], first[:], own, ALU.max)
+            if last:
+                for t in range(PACK):
+                    nc.vector.tensor_copy(second[:, t, :], y_win[t][:].indirect(part(n2_sb, c0, width)))
+            chosen = sb("chosen%d" % i, [P, PACK, width], BF16, tag="z_woven1" if last else None)
+            nc.vector.tensor_tensor(chosen[:], larger[:], second[:], ALU.min)
+            signed = sb("signed%d" % i, [P, PACK, width], BF16)
+            woven = sb("z_woven%d" % i, [P, width, PACK], BF16)
+            for t in range(PACK):
+                sign = gate_sign[:, t : t + 1]
+                if last:
+                    nc.vector.tensor_scalar(signed[:, t, :], chosen[:, t, :], sign, None, ALU.mult)
+                else:
+                    nc.scalar.activation(signed[:, t, :], chosen[:, t, :], ACT.Copy, scale=sign)
+            interleave(nc.vector.tensor_copy if last else nc.scalar.copy, woven[:], signed[:])
+            codes = sb("z_codes%d" % i, [P, width], U32)
+            scales = sb("z_scales%d" % i, [P, width], U8)
+            quantize(codes[:], scales[:], woven[:])
+            for t in range(PACK):
+                cols = slice(t * P, (t + 1) * P)
+                nc.tensor.matmul_mx(
+                    out=h_ps[t][:, c0 : c0 + width], lhsT=w1_dealt[:, cols].bitcast(FP8X4), lhsT_scale=w1_sc[:, cols],
+                    rhs=codes[:].bitcast(FP8X4), rhs_scale=scales[:], start=True, stop=True,
+                )
+            for t in range(PACK):
+                nc.scalar.copy(h_win[t][:, c0 : c0 + width], h_ps[t][:, c0 : c0 + width])
+
+        out_rows = out_0.rearrange("(p t) c -> p t c", t=PACK)
+        out_words = out_1[0].rearrange("p c r -> p (c r)").bitcast(I32)
+        out_scales = sb("out_scales", [P, H], U8)
+        for i, (c0, width) in enumerate(OUT_CHUNKS):
+            last = i == len(OUT_CHUNKS) - 1
+            cols = slice(c0, c0 + width)
+            weight = sb("weight%d" % i, [P, PACK, width], F32)
+            other = sb("other%d" % i, [P, PACK, width], F32)
+            for t in range(PACK):
+                nc.scalar.activation(weight[:, t, :], h_win[t][:].indirect(part(n3_sb, c0, width)), ACT.Sigmoid)
+                nc.vector.tensor_copy(other[:, t, :], h_win[t][:].indirect(part(n4_sb, c0, width)))
+            diff = sb("diff%d" % i, [P, PACK, width], F32)
+            for t in range(PACK):
+                nc.vector.tensor_tensor(diff[:, t, :], other[:, t, :], h_win[t][:, cols], ALU.subtract)
+            step = sb("step%d" % i, [P, PACK, width], F32)
+            nc.vector.tensor_tensor(step[:], diff[:], weight[:], ALU.mult)
+            mixed = sb("mixed%d" % i, [P, PACK, width], F32)
+            for t in range(PACK):
+                nc.vector.tensor_tensor(mixed[:, t, :], step[:, t, :], h_win[t][:, cols], ALU.add)
+            nc.sync.dma_start(out_rows[:, :, cols], mixed[:])
+            woven = sb("out_woven%d" % i, [P, width, PACK], BF16)
+            interleave(nc.vector.tensor_copy if last else nc.scalar.copy, woven[:], mixed[:])
+            codes = sb("out_codes%d" % i, [P, width], U32)
+            quantize(codes[:], out_scales[:, cols], woven[:])
+            nc.sync.dma_start(out_words[:, cols], codes[:].bitcast(I32))
+        for q in range(4):
+            queue = nc.scalar if q % 2 else nc.sync
+            queue.dma_start(
+                out_2[0, 4 * q : 4 * q + 4, :].bitcast(I32), out_scales[32 * q : 32 * q + 4, :].bitcast(I32)
+            )

@@ -19,7 +19,7 @@ P = 128
 PACK = 4
 WA_CHUNKS = ((0, 256), (256, 256))
 Z_CHUNKS = ((0, 256), (256, 128), (384, 128))
-OUT_CHUNKS = ((0, 256), (256, 128), (384, 128))
+OUT_CHUNKS = ((0, 128), (128, 256), (384, 128))
 
 
 def tile_picked_tokminmxtrack_none_po_kernel(
@@ -55,15 +55,15 @@ def tile_picked_tokminmxtrack_none_po_kernel(
         x_bytes = sb("x_bytes", [P, T], U8)
         nc.vector.memset(x_bytes[:].bitcast(I32), 0)
         offs_sb = load_list("offs_sb", offs)
+        gate = sb("gate", [P, PACK], F32)
+        nc.sync.dma_start(gate[:], gt.rearrange("(p t) o -> p (t o)", t=PACK))
+        wa_raw = sb("wa_raw", [P, PACK, H], F32)
+        wa_rows = wa.rearrange("(p t) c -> p t c", t=PACK)
+        nc.sync.dma_start(wa_raw[:, 0:2, :], wa_rows[:, 0:2, :])
+        load_scale_rows(nc.sync, x_bytes, x_scales[0])
+        nc.sync.dma_start(wa_raw[:, 2:4, :], wa_rows[:, 2:4, :])
         x_codes = sb("x_codes", [P, T], U32)
         nc.sync.dma_start(x_codes[:].bitcast(I32), x_words[0].rearrange("p c r -> p (c r)").bitcast(I32))
-        load_scale_rows(nc.sync, x_bytes, x_scales[0])
-        wa_rows = wa.rearrange("(p t) c -> p t c", t=PACK)
-        wa_raw = []
-        for i, (c0, width) in enumerate(WA_CHUNKS):
-            raw = sb("wa_raw%d" % i, [P, PACK, width], F32)
-            nc.sync.dma_start(raw[:], wa_rows[:, :, c0 : c0 + width])
-            wa_raw.append(raw)
 
         warm = sb("warm", [P, 2], F32)
         nc.vector.memset(warm[:, 0:1], 0.0)
@@ -71,8 +71,6 @@ def tile_picked_tokminmxtrack_none_po_kernel(
 
         w1_bytes = sb("w1_bytes", [P, N], U8)
         nc.vector.memset(w1_bytes[:].bitcast(I32), 0)
-        gate = sb("gate", [P, PACK], F32)
-        nc.sync.dma_start(gate[:], gt.rearrange("(p t) o -> p (t o)", t=PACK))
         n1_sb = load_list("n1_sb", n1)
         n2_sb = load_list("n2_sb", n2)
         w1_codes = sb("w1_codes", [P, N], U32)
@@ -88,35 +86,35 @@ def tile_picked_tokminmxtrack_none_po_kernel(
 
         tok_bytes = sb("tok_bytes", [P, S], U8)
         nc.vector.tensor_copy(tok_bytes[:], x_bytes[:].indirect(offs_sb[:]))
-        tok_codes = sb("tok_codes", [P, S], U32)
-        nc.vector.tensor_copy(tok_codes[:].rearrange("p (t m) -> p m t", t=PACK), x_codes[:].indirect(offs_sb[:]))
         tok_scales = sb("tok_scales", [P, S], U8)
         nc.vector.tensor_copy(
             tok_scales[:].rearrange("p (t m) -> p t m", t=PACK), tok_bytes[:].rearrange("p (m t) -> p t m", t=PACK)
         )
+        wa_mx = []
+        for i, (c0, width) in enumerate(WA_CHUNKS):
+            woven = sb("wa_woven%d" % i, [P, width, PACK], BF16)
+            interleave(nc.vector.tensor_copy if i else nc.scalar.copy, woven[:], wa_raw[:, :, c0 : c0 + width])
+            codes = sb("wa_codes%d" % i, [P, width], U32)
+            scales = sb("wa_scales%d" % i, [P, width], U8)
+            quantize(codes[:], scales[:], woven[:])
+            wa_mx.append((codes, scales))
+        tok_codes = sb("tok_codes", [P, S], U32)
+        nc.vector.tensor_copy(tok_codes[:].rearrange("p (t m) -> p m t", t=PACK), x_codes[:].indirect(offs_sb[:]))
 
         y_win = [sb("y_win%d" % t, [P, H], F32) for t in range(PACK)]
         y_own = [sb("y_own%d" % i, [P, PACK, w], BF16) for i, (c0, w) in enumerate(WA_CHUNKS)]
         y_ps = {}
-        for i, (c0, width) in enumerate(WA_CHUNKS):
-            woven = sb("wa_woven%d" % i, [P, width, PACK], BF16)
-            copy = nc.vector.tensor_copy if i == len(WA_CHUNKS) - 1 else nc.scalar.copy
-            interleave(copy, woven[:], wa_raw[i][:])
-            codes = sb("wa_codes%d" % i, [P, width], U32)
-            scales = sb("wa_scales%d" % i, [P, width], U8)
-            quantize(codes[:], scales[:], woven[:])
-            for t in range(PACK):
-                cols = slice(t * P, (t + 1) * P)
+        for t in range(PACK):
+            cols = slice(t * P, (t + 1) * P)
+            for i, (c0, width) in enumerate(WA_CHUNKS):
+                codes, scales = wa_mx[i]
                 acc = psum.tile([P, width], F32, name="y_ps", tag="bank%d" % (2 * t + i))
                 nc.tensor.matmul_mx(
                     out=acc[:], lhsT=tok_codes[:, cols].bitcast(FP8X4), lhsT_scale=tok_scales[:, cols],
                     rhs=codes[:].bitcast(FP8X4), rhs_scale=scales[:], start=True, stop=True,
                 )
                 y_ps[t, i] = acc
-            for t in range(PACK):
-                nc.scalar.activation(
-                    y_win[t][:, c0 : c0 + width], y_ps[t, i][:], ACT.Copy, scale=gate_abs[:, t : t + 1]
-                )
+                nc.scalar.activation(y_win[t][:, c0 : c0 + width], acc[:], ACT.Copy, scale=gate_abs[:, t : t + 1])
         for i in range(len(WA_CHUNKS)):
             for t in range(PACK):
                 nc.scalar.activation(y_own[i][:, t, :], y_ps[t, i][:], ACT.Copy, scale=gate_abs[:, t : t + 1])
@@ -148,16 +146,21 @@ def tile_picked_tokminmxtrack_none_po_kernel(
                 for t in range(PACK):
                     nc.vector.tensor_copy(second[:, t, :], y_win[t][:].indirect(part(n2_sb, c0, width)))
             chosen = sb("chosen%d" % i, [P, PACK, width], BF16, tag="z_woven1" if last else None)
-            nc.vector.tensor_tensor(chosen[:], larger[:], second[:], ALU.min)
-            signed = sb("signed%d" % i, [P, PACK, width], BF16)
+            for tiles in (slice(0, 3), slice(3, 4)) if last else (slice(0, 4),):
+                nc.vector.tensor_tensor(chosen[:, tiles, :], larger[:, tiles, :], second[:, tiles, :], ALU.min)
             woven = sb("z_woven%d" % i, [P, width, PACK], BF16)
-            for t in range(PACK):
-                sign = gate_sign[:, t : t + 1]
-                if last:
-                    nc.vector.tensor_scalar(signed[:, t, :], chosen[:, t, :], sign, None, ALU.mult)
-                else:
-                    nc.scalar.activation(signed[:, t, :], chosen[:, t, :], ACT.Copy, scale=sign)
-            interleave(nc.vector.tensor_copy if last else nc.scalar.copy, woven[:], signed[:])
+            if last:
+                nc.vector.tensor_tensor(
+                    woven[:].rearrange("p (c i) t -> p c t i", i=4),
+                    chosen[:].rearrange("p t (c i) -> p c t i", i=4),
+                    gate_sign[:].unsqueeze(1).unsqueeze(3).to_broadcast([P, width // 4, PACK, 4]),
+                    ALU.mult,
+                )
+            else:
+                signed = sb("signed%d" % i, [P, PACK, width], BF16)
+                for t in range(PACK):
+                    nc.scalar.activation(signed[:, t, :], chosen[:, t, :], ACT.Copy, scale=gate_sign[:, t : t + 1])
+                interleave(nc.scalar.copy, woven[:], signed[:])
             codes = sb("z_codes%d" % i, [P, width], U32)
             scales = sb("z_scales%d" % i, [P, width], U8)
             quantize(codes[:], scales[:], woven[:])
@@ -168,33 +171,53 @@ def tile_picked_tokminmxtrack_none_po_kernel(
                     rhs=codes[:].bitcast(FP8X4), rhs_scale=scales[:], start=True, stop=True,
                 )
             for t in range(PACK):
-                nc.scalar.copy(h_win[t][:, c0 : c0 + width], h_ps[t][:, c0 : c0 + width])
+                copy = nc.vector.tensor_copy if last and t > 0 else nc.scalar.copy
+                copy(h_win[t][:, c0 : c0 + width], h_ps[t][:, c0 : c0 + width])
 
         out_rows = out_0.rearrange("(p t) c -> p t c", t=PACK)
         out_words = out_1[0].rearrange("p c r -> p (c r)").bitcast(I32)
         out_scales = sb("out_scales", [P, H], U8)
+        pending = []
+
+        def hand_on(i, cols, woven, tag):
+            codes = sb("out_codes%d" % i, [P, cols.stop - cols.start], U32, tag=tag)
+            quantize(codes[:], out_scales[:, cols], woven[:])
+            nc.sync.dma_start(out_words[:, cols], codes[:].bitcast(I32))
+
         for i, (c0, width) in enumerate(OUT_CHUNKS):
             last = i == len(OUT_CHUNKS) - 1
             cols = slice(c0, c0 + width)
             weight = sb("weight%d" % i, [P, PACK, width], F32)
-            other = sb("other%d" % i, [P, PACK, width], F32)
-            for t in range(PACK):
-                nc.scalar.activation(weight[:, t, :], h_win[t][:].indirect(part(n3_sb, c0, width)), ACT.Sigmoid)
-                nc.vector.tensor_copy(other[:, t, :], h_win[t][:].indirect(part(n4_sb, c0, width)))
-            diff = sb("diff%d" % i, [P, PACK, width], F32)
-            for t in range(PACK):
-                nc.vector.tensor_tensor(diff[:, t, :], other[:, t, :], h_win[t][:, cols], ALU.subtract)
-            step = sb("step%d" % i, [P, PACK, width], F32)
-            nc.vector.tensor_tensor(step[:], diff[:], weight[:], ALU.mult)
+            taken = sb("taken%d" % i, [P, PACK, width], F32)
+            left = sb("left%d" % i, [P, PACK, width], F32)
             mixed = sb("mixed%d" % i, [P, PACK, width], F32)
             for t in range(PACK):
-                nc.vector.tensor_tensor(mixed[:, t, :], step[:, t, :], h_win[t][:, cols], ALU.add)
+                nc.scalar.activation(weight[:, t, :], h_win[t][:].indirect(part(n3_sb, c0, width)), ACT.Sigmoid)
+                nc.vector.scalar_tensor_tensor(
+                    left[:, t, :], weight[:, t, :], 1.0, h_win[t][:, cols], ALU.subtract, ALU.mult
+                )
+                nc.vector.tensor_tensor(
+                    taken[:, t, :], h_win[t][:].indirect(part(n4_sb, c0, width)), weight[:, t, :], ALU.mult
+                )
+                if last:
+                    nc.vector.tensor_tensor(mixed[:, t, :], taken[:, t, :], left[:, t, :], ALU.subtract)
+            if not last:
+                nc.vector.tensor_tensor(mixed[:], taken[:], left[:], ALU.subtract)
             nc.sync.dma_start(out_rows[:, :, cols], mixed[:])
             woven = sb("out_woven%d" % i, [P, width, PACK], BF16)
-            interleave(nc.vector.tensor_copy if last else nc.scalar.copy, woven[:], mixed[:])
-            codes = sb("out_codes%d" % i, [P, width], U32)
-            quantize(codes[:], out_scales[:, cols], woven[:])
-            nc.sync.dma_start(out_words[:, cols], codes[:].bitcast(I32))
+            if last:
+                nc.vector.tensor_tensor(
+                    woven[:].rearrange("p (c i) t -> p c t i", i=4),
+                    taken[:].rearrange("p t (c i) -> p c t i", i=4),
+                    left[:].rearrange("p t (c i) -> p c t i", i=4),
+                    ALU.subtract,
+                )
+            else:
+                interleave(nc.scalar.copy, woven[:], mixed[:])
+            if pending:
+                hand_on(*pending.pop(), "weight%d" % i)
+            pending.append((i, cols, woven))
+        hand_on(*pending.pop(), None)
         for q in range(4):
             queue = nc.scalar if q % 2 else nc.sync
             queue.dma_start(

from contextlib import ExitStack

import concourse.mybir as mybir

K, T, S, N, H = 512, 2048, 512, 512, 512
FLOPS = 2 * K * S * H + 2 * S * N * H

F32 = mybir.dt.float32
BF16 = mybir.dt.bfloat16
I32 = mybir.dt.int32
U32 = mybir.dt.uint32
U16 = mybir.dt.uint16
U8 = mybir.dt.uint8
FP8X4 = mybir.dt.float8_e4m3fn_x4
ALU = mybir.AluOpType
ACT = mybir.ActivationFunctionType

P = 128
PACK = 4
WA_CHUNKS = ((0, 256), (256, 256))
Z_CHUNKS = ((0, 256), (256, 128), (384, 128))
OUT_CHUNKS = ((0, 128), (128, 256), (384, 128))


def tile_picked_tokminmxtrack_none_po_kernel(
    tc, x_words, x_scales, wa, gt, w1_words, w1_scales, offs, n1, n2, n3, n4, out_0, out_1, out_2
):
    nc = tc.nc
    with ExitStack() as ctx:
        keep = ctx.enter_context(tc.tile_pool(name="keep", bufs=1))
        psum = ctx.enter_context(tc.psum_pool(name="psum", bufs=1))

        def sb(name, shape, dtype, tag=None):
            return keep.tile(shape, dtype, name=name, tag=tag or name, align_bytes=64)

        def load_list(name, src):
            tile = keep.tile([P, S // 16], U16, name=name)
            nc.sync.dma_start(tile[:], src)
            return tile

        def part(lists, c0, width):
            return lists[:, c0 // 16 : (c0 + width) // 16]

        def load_scale_rows(queue, tile, rows):
            by_row = rows.rearrange("(q r) c -> r q c", r=PACK)
            for r in range(PACK):
                queue.dma_start(tile[r:P:32, :].bitcast(I32), by_row[r].bitcast(I32))

        def interleave(copy, dst, src):
            copy(dst.rearrange("p (c i) t -> p c t i", i=4), src.rearrange("p t (c i) -> p c t i", i=4))

        def quantize(codes, scales, woven):
            nc.vector.quantize_mx(out=codes.bitcast(FP8X4), scales=scales, in_=woven.rearrange("p c t -> p (c t)"))

        x_bytes = sb("x_bytes", [P, T], U8)
        nc.vector.memset(x_bytes[:].bitcast(I32), 0)
        offs_sb = load_list("offs_sb", offs)
        gate = sb("gate", [P, PACK], F32)
        nc.sync.dma_start(gate[:], gt.rearrange("(p t) o -> p (t o)", t=PACK))
        wa_raw = sb("wa_raw", [P, PACK, H], F32)
        wa_rows = wa.rearrange("(p t) c -> p t c", t=PACK)
        nc.sync.dma_start(wa_raw[:, 0:2, :], wa_rows[:, 0:2, :])
        load_scale_rows(nc.sync, x_bytes, x_scales[0])
        nc.sync.dma_start(wa_raw[:, 2:4, :], wa_rows[:, 2:4, :])
        x_codes = sb("x_codes", [P, T], U32)
        nc.sync.dma_start(x_codes[:].bitcast(I32), x_words[0].rearrange("p c r -> p (c r)").bitcast(I32))

        warm = sb("warm", [P, 2], F32)
        nc.vector.memset(warm[:, 0:1], 0.0)
        nc.scalar.activation(warm[:, 1:2], warm[:, 0:1], ACT.Sigmoid)

        w1_bytes = sb("w1_bytes", [P, N], U8)
        nc.vector.memset(w1_bytes[:].bitcast(I32), 0)
        n1_sb = load_list("n1_sb", n1)
        n2_sb = load_list("n2_sb", n2)
        w1_codes = sb("w1_codes", [P, N], U32)
        nc.sync.dma_start(w1_codes[:].bitcast(I32), w1_words[0].rearrange("p c r -> p (c r)").bitcast(I32))
        load_scale_rows(nc.sync, w1_bytes, w1_scales[0])
        n3_sb = load_list("n3_sb", n3)
        n4_sb = load_list("n4_sb", n4)

        gate_abs = sb("gate_abs", [P, PACK], F32)
        gate_sign = sb("gate_sign", [P, PACK], F32)
        nc.scalar.activation(gate_abs[:], gate[:], ACT.Abs)
        nc.scalar.activation(gate_sign[:], gate[:], ACT.Sign)

        tok_bytes = sb("tok_bytes", [P, S], U8)
        nc.vector.tensor_copy(tok_bytes[:], x_bytes[:].indirect(offs_sb[:]))
        tok_scales = sb("tok_scales", [P, S], U8)
        nc.vector.tensor_copy(
            tok_scales[:].rearrange("p (t m) -> p t m", t=PACK), tok_bytes[:].rearrange("p (m t) -> p t m", t=PACK)
        )
        wa_mx = []
        for i, (c0, width) in enumerate(WA_CHUNKS):
            woven = sb("wa_woven%d" % i, [P, width, PACK], BF16)
            interleave(nc.vector.tensor_copy if i else nc.scalar.copy, woven[:], wa_raw[:, :, c0 : c0 + width])
            codes = sb("wa_codes%d" % i, [P, width], U32)
            scales = sb("wa_scales%d" % i, [P, width], U8)
            quantize(codes[:], scales[:], woven[:])
            wa_mx.append((codes, scales))
        tok_codes = sb("tok_codes", [P, S], U32)
        nc.vector.tensor_copy(tok_codes[:].rearrange("p (t m) -> p m t", t=PACK), x_codes[:].indirect(offs_sb[:]))

        y_win = [sb("y_win%d" % t, [P, H], F32) for t in range(PACK)]
        y_own = [sb("y_own%d" % i, [P, PACK, w], BF16) for i, (c0, w) in enumerate(WA_CHUNKS)]
        y_ps = {}
        for t in range(PACK):
            cols = slice(t * P, (t + 1) * P)
            for i, (c0, width) in enumerate(WA_CHUNKS):
                codes, scales = wa_mx[i]
                acc = psum.tile([P, width], F32, name="y_ps", tag="bank%d" % (2 * t + i))
                nc.tensor.matmul_mx(
                    out=acc[:], lhsT=tok_codes[:, cols].bitcast(FP8X4), lhsT_scale=tok_scales[:, cols],
                    rhs=codes[:].bitcast(FP8X4), rhs_scale=scales[:], start=True, stop=True,
                )
                y_ps[t, i] = acc
                nc.scalar.activation(y_win[t][:, c0 : c0 + width], acc[:], ACT.Copy, scale=gate_abs[:, t : t + 1])
        for i in range(len(WA_CHUNKS)):
            for t in range(PACK):
                nc.scalar.activation(y_own[i][:, t, :], y_ps[t, i][:], ACT.Copy, scale=gate_abs[:, t : t + 1])

        w1_dealt = sb("w1_dealt", [P, N], U32)
        nc.vector.tensor_copy(
            w1_dealt[:].bitcast(I32).rearrange("p (t m) -> p m t", t=PACK),
            w1_codes[:].bitcast(I32).rearrange("p (m t) -> p m t", t=PACK),
        )
        w1_sc = sb("w1_sc", [P, N], U8)
        nc.vector.tensor_copy(
            w1_sc[:].rearrange("p (t m) -> p t m", t=PACK), w1_bytes[:].rearrange("p (m t) -> p t m", t=PACK)
        )

        h_win = [sb("h_win%d" % t, [P, H], F32) for t in range(PACK)]
        h_ps = [psum.tile([P, H], F32, name="h_ps", tag="bank%d" % (2 * t)) for t in range(PACK)]
        for i, (c0, width) in enumerate(Z_CHUNKS):
            last = i == len(Z_CHUNKS) - 1
            first = sb("first%d" % i, [P, PACK, width], BF16, tag="first")
            second = sb("second%d" % i, [P, PACK, width], BF16, tag="z_woven0" if last else "second")
            for t in range(PACK):
                nc.vector.tensor_copy(first[:, t, :], y_win[t][:].indirect(part(n1_sb, c0, width)))
                if not last:
                    nc.vector.tensor_copy(second[:, t, :], y_win[t][:].indirect(part(n2_sb, c0, width)))
            own = y_own[c0 // 256][:, :, c0 % 256 : c0 % 256 + width]
            larger = sb("larger%d" % i, [P, PACK, width], BF16)
            nc.vector.tensor_tensor(larger[:], first[:], own, ALU.max)
            if last:
                for t in range(PACK):
                    nc.vector.tensor_copy(second[:, t, :], y_win[t][:].indirect(part(n2_sb, c0, width)))
            chosen = sb("chosen%d" % i, [P, PACK, width], BF16, tag="z_woven1" if last else None)
            for tiles in (slice(0, 3), slice(3, 4)) if last else (slice(0, 4),):
                nc.vector.tensor_tensor(chosen[:, tiles, :], larger[:, tiles, :], second[:, tiles, :], ALU.min)
            woven = sb("z_woven%d" % i, [P, width, PACK], BF16)
            if last:
                nc.vector.tensor_tensor(
                    woven[:].rearrange("p (c i) t -> p c t i", i=4),
                    chosen[:].rearrange("p t (c i) -> p c t i", i=4),
                    gate_sign[:].unsqueeze(1).unsqueeze(3).to_broadcast([P, width // 4, PACK, 4]),
                    ALU.mult,
                )
            else:
                signed = sb("signed%d" % i, [P, PACK, width], BF16)
                for t in range(PACK):
                    nc.scalar.activation(signed[:, t, :], chosen[:, t, :], ACT.Copy, scale=gate_sign[:, t : t + 1])
                interleave(nc.scalar.copy, woven[:], signed[:])
            codes = sb("z_codes%d" % i, [P, width], U32)
            scales = sb("z_scales%d" % i, [P, width], U8)
            quantize(codes[:], scales[:], woven[:])
            for t in range(PACK):
                cols = slice(t * P, (t + 1) * P)
                nc.tensor.matmul_mx(
                    out=h_ps[t][:, c0 : c0 + width], lhsT=w1_dealt[:, cols].bitcast(FP8X4), lhsT_scale=w1_sc[:, cols],
                    rhs=codes[:].bitcast(FP8X4), rhs_scale=scales[:], start=True, stop=True,
                )
            for t in range(PACK):
                copy = nc.vector.tensor_copy if last and t > 0 else nc.scalar.copy
                copy(h_win[t][:, c0 : c0 + width], h_ps[t][:, c0 : c0 + width])

        out_rows = out_0.rearrange("(p t) c -> p t c", t=PACK)
        out_words = out_1[0].rearrange("p c r -> p (c r)").bitcast(I32)
        out_scales = sb("out_scales", [P, H], U8)
        pending = []

        def hand_on(i, cols, woven, tag):
            codes = sb("out_codes%d" % i, [P, cols.stop - cols.start], U32, tag=tag)
            quantize(codes[:], out_scales[:, cols], woven[:])
            nc.sync.dma_start(out_words[:, cols], codes[:].bitcast(I32))

        for i, (c0, width) in enumerate(OUT_CHUNKS):
            last = i == len(OUT_CHUNKS) - 1
            cols = slice(c0, c0 + width)
            weight = sb("weight%d" % i, [P, PACK, width], F32)
            taken = sb("taken%d" % i, [P, PACK, width], F32)
            left = sb("left%d" % i, [P, PACK, width], F32)
            mixed = sb("mixed%d" % i, [P, PACK, width], F32)
            for t in range(PACK):
                nc.scalar.activation(weight[:, t, :], h_win[t][:].indirect(part(n3_sb, c0, width)), ACT.Sigmoid)
                nc.vector.scalar_tensor_tensor(
                    left[:, t, :], weight[:, t, :], 1.0, h_win[t][:, cols], ALU.subtract, ALU.mult
                )
                nc.vector.tensor_tensor(
                    taken[:, t, :], h_win[t][:].indirect(part(n4_sb, c0, width)), weight[:, t, :], ALU.mult
                )
                if last:
                    nc.vector.tensor_tensor(mixed[:, t, :], taken[:, t, :], left[:, t, :], ALU.subtract)
            if not last:
                nc.vector.tensor_tensor(mixed[:], taken[:], left[:], ALU.subtract)
            nc.sync.dma_start(out_rows[:, :, cols], mixed[:])
            woven = sb("out_woven%d" % i, [P, width, PACK], BF16)
            if last:
                nc.vector.tensor_tensor(
                    woven[:].rearrange("p (c i) t -> p c t i", i=4),
                    taken[:].rearrange("p t (c i) -> p c t i", i=4),
                    left[:].rearrange("p t (c i) -> p c t i", i=4),
                    ALU.subtract,
                )
            else:
                interleave(nc.scalar.copy, woven[:], mixed[:])
            if pending:
                hand_on(*pending.pop(), "weight%d" % i)
            pending.append((i, cols, woven))
        hand_on(*pending.pop(), None)
        for q in range(4):
            queue = nc.scalar if q % 2 else nc.sync
            queue.dma_start(
                out_2[0, 4 * q : 4 * q + 4, :].bitcast(I32), out_scales[32 * q : 32 * q + 4, :].bitcast(I32)
            )
